import numpy as np
import ml_dtypes


def mxq(x, axis, fmt="e4m3"):
    dtype, down = {"e4m3": (ml_dtypes.float8_e4m3fn, 7), "e5m2": (ml_dtypes.float8_e5m2, 14)}[fmt]
    v = np.moveaxis(np.asarray(x, np.float32).astype(ml_dtypes.bfloat16).astype(np.float64), axis, -1)
    blocks = v.reshape(v.shape[:-1] + (-1, 32))
    amax = np.abs(blocks).max(-1, keepdims=True)
    byte = np.maximum(np.where(amax > 0, np.frexp(amax)[1] - 1 + 127, 0) - down, 1)
    scale = np.exp2(byte - 127.0)
    codes = (blocks / scale).astype(np.float32).astype(dtype).astype(np.float64)
    return np.moveaxis((codes * scale).reshape(v.shape), -1, axis)


WIDE = False


def mx_kscale(k):
    if not WIDE:
        return np.ones(k)
    levels = np.array([10, -10, 5, -5, 0])
    if k % 512:
        return np.exp2(np.random.permutation(np.resize(levels, k // 32))).repeat(32)
    a = np.empty((k // 512, 16))
    for p in range(k // 512):
        a[p, :8] = np.random.permutation(np.resize(levels, 8))
        for g in range(8):
            far = levels[np.abs(levels - a[p, g]) >= 10]
            a[p, g + 8] = far[np.random.randint(len(far))]
    return np.exp2(a.ravel()).repeat(32)


def f64(x):
    return np.asarray(x).astype(np.float64)


def striped(idx):
    return np.tile(idx.reshape(-1, 16).T, (8, 1)).astype(np.uint16)


def unstriped(offs):
    return offs[:16].T.reshape(-1).astype(np.int64)


E2M1 = np.array([0.0, 0.5, 1.0, 1.5, 2.0, 3.0, 4.0, 6.0, -0.0, -0.5, -1.0, -1.5, -2.0, -3.0, -4.0, -6.0])


def pack_weight(w, fmt):
    k, n = w.shape
    w = f64(np.asarray(w, np.float32).astype(ml_dtypes.bfloat16)).reshape(k // 32, 32, n)
    amax = np.abs(w).max(1)
    if fmt == "e4m3":
        byte = np.frexp(amax)[1] - 1 + 127 - 7
    else:
        mant, ex = np.frexp(amax / 6.0)
        byte = np.where(mant > 0.5, ex, ex - 1) + 127
    byte = np.clip(np.where(amax > 0, byte, 1), 1, 254)
    scaled = (w * np.exp2(127.0 - byte)[:, None, :]).reshape(k, n).astype(np.float32)
    by_word = np.ascontiguousarray(scaled.reshape(k // 512, 128, 4, n).transpose(0, 1, 3, 2))
    if fmt == "e4m3":
        words = by_word.astype(ml_dtypes.float8_e4m3fn).view(np.uint8)
    else:
        c = by_word.astype(ml_dtypes.float4_e2m1fn).view(np.uint8) & 0xF
        words = (c[..., 0::2] | (c[..., 1::2] << 4)).reshape(k // 512, 128, 2 * n)
    return np.ascontiguousarray(words), np.ascontiguousarray(byte.astype(np.uint8).reshape(k // 512, 16, n))


def unpack_weight(words, scales, fmt):
    g, _, n = scales.shape
    words = np.ascontiguousarray(words).reshape(g, 128, n, -1)
    if fmt == "e4m3":
        vals = words.view(ml_dtypes.float8_e4m3fn).astype(np.float64)
    else:
        nib = np.empty((g, 128, n, 4), np.uint8)
        nib[..., 0::2] = words & 0xF
        nib[..., 1::2] = words >> 4
        vals = E2M1[nib]
    vals = vals * np.repeat(np.exp2(scales.astype(np.float64) - 127.0), 8, axis=1)[..., None]
    return vals.transpose(0, 1, 3, 2).reshape(g * 512, n)


def sigmoid(v):
    return 1.0 / (1.0 + np.exp(-np.maximum(v, -700.0)))


K, T, E, C, H, N = 512, 1024, 16, 128, 512, 128
TOP = 4
PAD = 64


def by_expert(wq, xq):
    return np.concatenate([wq[e].T @ xq[:, e * C:(e + 1) * C] for e in range(E)], axis=1)


def setup_inputs():
    n = np.random.standard_normal
    s = mx_kscale(K)[:, None]
    u = mx_kscale(H)
    slot_token = np.empty(E * C, np.int64); pos = np.tile(E * C + np.arange(T) % PAD, (TOP, 1)); taken = np.zeros(T, np.int64)
    liked = np.random.randn(T)
    for e in np.random.permutation(E):
        free = np.flatnonzero(taken < TOP); pick = np.random.permutation(free[np.argsort(-(liked[free] + np.random.gumbel(size=free.size)))[:C]]); slot_token[e * C:(e + 1) * C] = pick
        pos[taken[pick], pick] = e * C + np.arange(C); taken[pick] += 1
    g = np.random.uniform(0.2, 0.8, (TOP, T))
    x = pack_weight(n((K, T)) * s, "e4m3")
    return {
        "x_words": x[0],
        "x_scales": x[1],
        "w1": (n((E, K, H)) / np.sqrt(K) / s[None]).astype(np.float32),
        "w3": (n((E, K, H)) / np.sqrt(K) / s[None] * u[None, None, :]).astype(np.float32),
        "w2": (n((E, H, N)) / np.sqrt(H) / u[None, :, None]).astype(np.float32),
        "gate": np.stack([np.tile(r, (N, 1)) for r in g]).astype(np.float32),
        "offs": striped(slot_token),
        "pos1": striped(pos[0]),
        "pos2": striped(pos[1]),
        "pos3": striped(pos[2]),
        "pos4": striped(pos[3]),
    }


def reference(x_words, x_scales, w1, w3, w2, gate, offs, pos1, pos2, pos3, pos4):
    idx = unstriped(offs)
    xq = unpack_weight(x_words, x_scales, "e4m3")[:, idx]
    h = sigmoid(by_expert(mxq(f64(w1), 1, "e4m3"), xq))
    h = h * by_expert(mxq(f64(w3), 1, "e4m3"), xq)
    y = by_expert(mxq(f64(w2), 1, "e4m3"), mxq(h, 0, "e4m3"))
    y = np.concatenate([y, np.zeros((N, PAD))], axis=1)
    return sum(f64(gate[r]) * y[:, unstriped(p)] for r, p in enumerate((pos1, pos2, pos3, pos4)))

@@ -1,0 +1,223 @@
+from contextlib import ExitStack
+
+import concourse.mybir as mybir
+from concourse.masks import make_identity
+
+K, T, E, C, H, N = 512, 1024, 16, 128, 512, 128
+TOP = 4
+PAD = 64
+SLOTS = E * C
+
+FLOPS = 2 * SLOTS * (2 * K * H + H * N)
+
+F32 = mybir.dt.float32
+BF16 = mybir.dt.bfloat16
+I32 = mybir.dt.int32
+U32 = mybir.dt.uint32
+U16 = mybir.dt.uint16
+U8 = mybir.dt.uint8
+FP8X4 = mybir.dt.float8_e4m3fn_x4
+MULT = mybir.AluOpType.mult
+ADD = mybir.AluOpType.add
+SIGMOID = mybir.ActivationFunctionType.Sigmoid
+
+P = 128
+PACK = 4
+STRIPE = 16
+GATHER_EXPERTS = 4
+RING = 12
+HALF = T // 2
+W2_PIECES = ((0, 4, 5), (4, 8, 9), (8, 12, 15), (12, 14, 15), (14, 15, 15), (15, 16, 15))
+
+
+def tile_moe_ecr_glu_sigmoid_kernel(
+    tc, x_words, x_scales, w1, w3, w2, gate, offs, pos1, pos2, pos3, pos4, out
+):
+    nc = tc.nc
+    with ExitStack() as ctx:
+        keep = ctx.enter_context(tc.tile_pool(name="keep", bufs=1))
+        ring = ctx.enter_context(tc.tile_pool(name="ring", bufs=RING))
+        work = ctx.enter_context(tc.tile_pool(name="work", bufs=4))
+        psum = ctx.enter_context(tc.psum_pool(name="psum", bufs=2))
+
+        token_words = keep.tile([P, T], I32, name="token_words", align_bytes=64)
+        token_scales = keep.tile([P, T], U8, name="token_scales", align_bytes=64)
+        slot_list = keep.tile([P, SLOTS // STRIPE], U16, name="slot_list")
+        scale_rows = keep.tile([P, T // 4], I32, name="scale_rows")
+        nc.gpsimd.memset(token_scales[:].bitcast(I32), 0)
+        nc.sync.dma_start(out=token_words[:], in_=x_words[0].rearrange("p t r -> p (t r)").bitcast(I32))
+        nc.sync.dma_start(slot_list[:], offs)
+        for r in range(4):
+            nc.sync.dma_start(out=scale_rows[r:P:32, :], in_=x_scales[0, r:16:4, :].bitcast(I32))
+        for q in range(4):
+            live = slice(32 * q, 32 * q + 4)
+            nc.vector.tensor_copy(token_scales[live, :].bitcast(I32), scale_rows[live, :])
+
+        raw1, raw3, raw2 = {}, {}, {}
+        pos_lists = []
+        for e in range(E):
+            raw1[e] = ring.tile([P, PACK, H], F32, name="raw1", tag="ring", align_bytes=64)
+            nc.sync.dma_start(out=raw1[e][:], in_=w1[e].rearrange("(p j) c -> p j c", j=PACK))
+            raw3[e] = ring.tile([P, PACK, H], F32, name="raw3", tag="ring", align_bytes=64)
+            nc.sync.dma_start(out=raw3[e][:], in_=w3[e].rearrange("(p j) c -> p j c", j=PACK))
+            if e == 0:
+                for r, pos in enumerate((pos1, pos2, pos3, pos4)):
+                    pos_list = keep.tile([P, T // STRIPE], U16, name="pos_list%d" % r)
+                    nc.sync.dma_start(pos_list[:], pos)
+                    pos_lists.append(pos_list)
+            for first, end, after in W2_PIECES:
+                if after == e:
+                    piece = ring.tile([P, end - first, PACK * N], F32, name="raw2", tag="ring", align_bytes=64)
+                    nc.sync.dma_start(
+                        out=piece[:], in_=w2[first:end].rearrange("e (p j) n -> p e (j n)", j=PACK)
+                    )
+                    for i in range(first, end):
+                        raw2[i] = piece[:, i - first, :]
+        gates = {}
+        for half in range(2):
+            late = ring.tile([P, TOP - 1, HALF], F32, name="gate_late", tag="ring", align_bytes=64)
+            nc.sync.dma_start(
+                out=late[:], in_=gate[1:TOP, :, half * HALF : (half + 1) * HALF].rearrange("r p t -> p r t")
+            )
+            for r in range(1, TOP):
+                gates[r, half] = late[:, r - 1, :]
+        gate_first = ring.tile([P, T], F32, name="gate_first", tag="ring", align_bytes=64)
+        nc.sync.dma_start(out=gate_first[:], in_=gate[0])
+        for half in range(2):
+            gates[0, half] = gate_first[:, half * HALF : (half + 1) * HALF]
+
+        identity = keep.tile([P, P], F32, name="identity")
+        make_identity(nc, identity[:])
+        y_slots = keep.tile([P, SLOTS + PAD], F32, name="y_slots")
+        nc.gpsimd.memset(y_slots[:, SLOTS:], 0.0)
+
+        slot_words, slot_scales = {}, {}
+
+        def gather_tokens(q):
+            width = GATHER_EXPERTS * C
+            entries = slot_list[:, q * width // STRIPE : (q + 1) * width // STRIPE]
+            slot_words[q] = keep.tile([P, width], U32, name="slot_words%d" % q, align_bytes=64)
+            slot_scales[q] = keep.tile([P, width], U8, name="slot_scales%d" % q, align_bytes=64)
+            nc.vector.tensor_copy(slot_words[q][:], token_words[:].bitcast(U32).indirect(entries))
+            nc.vector.tensor_copy(slot_scales[q][:], token_scales[:].indirect(entries))
+
+        def round_first_layer(copy, raw, name):
+            grouped = work.tile([P, PACK * H], BF16, name=name, align_bytes=64, bufs=3)
+            copy(
+                grouped[:].rearrange("p (t a b j) -> p a j b t", t=PACK, b=2, j=PACK),
+                raw[:].rearrange("p j (a b t) -> p a j b t", b=2, t=PACK),
+            )
+            return grouped[:]
+
+        def quantize(pool, grouped, width, name, bufs):
+            codes = pool.tile([P, width], U32, name=name + "_codes", align_bytes=64, bufs=bufs)
+            scales = pool.tile([P, width], U8, name=name + "_scales", align_bytes=64, bufs=bufs)
+            nc.vector.quantize_mx(out=codes[:].bitcast(FP8X4), scales=scales[:], in_=grouped)
+            return codes, scales
+
+        def first_layer_product(e, weights, name):
+            codes, scales = weights
+            q, place = divmod(e, GATHER_EXPERTS)
+            slots = slice(place * C, (place + 1) * C)
+            bank = psum.tile([P, PACK, C], F32, name=name)
+            for t in range(PACK):
+                cols = slice(t * P, (t + 1) * P)
+                nc.tensor.matmul_mx(
+                    out=bank[:, t, :],
+                    lhsT=codes[:, cols].bitcast(FP8X4),
+                    lhsT_scale=scales[:, cols],
+                    rhs=slot_words[q][:, slots].bitcast(FP8X4),
+                    rhs_scale=slot_scales[q][:, slots],
+                    start=True,
+                    stop=True,
+                )
+            return bank
+
+        hidden = {}
+
+        banks = {}
+
+        def first_layer(e):
+            grouped1 = round_first_layer(nc.scalar.copy, raw1[e], "grouped1")
+            grouped3 = round_first_layer(nc.vector.tensor_copy, raw3[e], "grouped3")
+            if e > 0:
+                gated_unit(e - 1, raw1[e][:, 0, :], raw3[e][:, 0, : C * PACK // 2].bitcast(BF16))
+            banks[e] = (
+                first_layer_product(e, quantize(work, grouped1, H, "w1", 2), "a_bank"),
+                first_layer_product(e, quantize(work, grouped3, H, "w3", 2), "b_bank"),
+            )
+
+        def gated_unit(e, sig, h):
+            a_bank, b_bank = banks[e]
+            sig_view = sig.rearrange("p (s t) -> p s t", t=PACK)
+            nc.scalar.activation(sig_view, a_bank[:].rearrange("p t s -> p s t"), SIGMOID)
+            nc.vector.tensor_tensor(
+                h.rearrange("p (s t) -> p s t", t=PACK), b_bank[:].rearrange("p t s -> p s t"), sig_view, MULT
+            )
+            hidden[e] = quantize(keep, h, C, "h%d" % e, 1)
+
+        def second_layer(first, end):
+            bank = psum.tile([P, end - first, C], F32, name="y_bank")
+            for e in range(first, end):
+                grouped = work.tile([P, PACK * N], BF16, name="grouped2", align_bytes=64)
+                copy = nc.vector.tensor_copy if e >= E // 2 and e % 2 == 1 else nc.scalar.copy
+                copy(
+                    grouped[:].rearrange("p (a i j) -> p a j i", i=4, j=PACK),
+                    raw2[e].rearrange("p (j a i) -> p a j i", j=PACK, i=4),
+                )
+                codes, scales = quantize(work, grouped[:], N, "w2", 4)
+                nc.tensor.matmul_mx(
+                    out=bank[:, e - first, :],
+                    lhsT=codes[:].bitcast(FP8X4),
+                    lhsT_scale=scales[:],
+                    rhs=hidden[e][0][:].bitcast(FP8X4),
+                    rhs_scale=hidden[e][1][:],
+                    start=True,
+                    stop=True,
+                )
+            nc.scalar.copy(y_slots[:, first * C : end * C], bank[:].rearrange("p e s -> p (e s)"))
+
+        for e in range(E):
+            if e % GATHER_EXPERTS == 0:
+                gather_tokens(e // GATHER_EXPERTS)
+            first_layer(e)
+            if e == E - 1:
+                last_sig = keep.tile([P, C * PACK], F32, name="last_sig")
+                last_h = keep.tile([P, C * PACK], BF16, name="last_h", align_bytes=64)
+                gated_unit(e, last_sig[:], last_h[:])
+            for first, end, after in W2_PIECES:
+                if after == e:
+                    second_layer(first, end)
+
+        def gated(r, half):
+            product = keep.tile([P, HALF], F32, name="product%d_%d" % (r, half))
+            entries = pos_lists[r][:, half * HALF // STRIPE : (half + 1) * HALF // STRIPE]
+            nc.vector.tensor_tensor(product[:], y_slots[:].indirect(entries), gates[r, half], MULT)
+            return product
+
+        blocks = HALF // P
+        partial = {}
+        for half in range(2):
+            turned = psum.tile([P, blocks, P], F32, name="a_bank")
+            order = list(range(TOP - 1, 0, -1))
+            for r in order:
+                product = gated(r, half)
+                for b in range(blocks):
+                    nc.tensor.matmul(
+                        turned[:, b, :],
+                        product[:, b * P : (b + 1) * P],
+                        identity[:],
+                        start=(r == order[0] and b == 0),
+                        stop=(r == order[-1] and b == blocks - 1),
+                        is_transpose=True,
+                    )
+            turned_sum = work.tile([P, blocks, P], F32, name="turned_sum", bufs=2)
+            nc.scalar.copy(turned_sum[:], turned[:])
+            partial[half] = psum.tile([P, blocks, P], F32, name="b_bank")
+            for b in range(blocks):
+                nc.tensor.transpose(partial[half][:, b, :], turned_sum[:, b, :], identity[:])
+        for half in range(2):
+            product = gated(0, half)
+            result = work.tile([P, HALF], F32, name="result", bufs=2)
+            nc.vector.tensor_tensor(result[:], partial[half][:].rearrange("p b t -> p (b t)"), product[:], ADD)
+            nc.sync.dma_start(out=out[:, half * HALF : (half + 1) * HALF], in_=result[:])

@@ -27,7 +27,8 @@ STRIPE = 16
 GATHER_EXPERTS = 4
 RING = 12
 HALF = T // 2
-W2_PIECES = ((0, 4, 5), (4, 8, 9), (8, 12, 15), (12, 14, 15), (14, 15, 15), (15, 16, 15))
+W2_LOADS = tuple((e, e + 2) for e in range(0, E - 2, 2)) + ((E - 2, E - 1), (E - 1, E))
+Y_BANKS = ((0, 4), (4, 8), (8, 12), (12, 14), (14, 16))
 
 
 def tile_moe_ecr_glu_sigmoid_kernel(
@@ -56,23 +57,20 @@ def tile_moe_ecr_glu_sigmoid_kernel(
         raw1, raw3, raw2 = {}, {}, {}
         pos_lists = []
         for e in range(E):
-            raw1[e] = ring.tile([P, PACK, H], F32, name="raw1", tag="ring", align_bytes=64)
-            nc.sync.dma_start(out=raw1[e][:], in_=w1[e].rearrange("(p j) c -> p j c", j=PACK))
-            raw3[e] = ring.tile([P, PACK, H], F32, name="raw3", tag="ring", align_bytes=64)
-            nc.sync.dma_start(out=raw3[e][:], in_=w3[e].rearrange("(p j) c -> p j c", j=PACK))
+            for raw, w in ((raw1, w1), (raw3, w3)):
+                piece = ring.tile([P, PACK * H], F32, name="raw", tag="ring", align_bytes=64)
+                nc.sync.dma_start(out=piece[:], in_=w[e].rearrange("(p j) c -> p (j c)", j=PACK))
+                raw[e] = piece[:]
             if e == 0:
                 for r, pos in enumerate((pos1, pos2, pos3, pos4)):
                     pos_list = keep.tile([P, T // STRIPE], U16, name="pos_list%d" % r)
                     nc.sync.dma_start(pos_list[:], pos)
                     pos_lists.append(pos_list)
-            for first, end, after in W2_PIECES:
-                if after == e:
-                    piece = ring.tile([P, end - first, PACK * N], F32, name="raw2", tag="ring", align_bytes=64)
-                    nc.sync.dma_start(
-                        out=piece[:], in_=w2[first:end].rearrange("e (p j) n -> p e (j n)", j=PACK)
-                    )
-                    for i in range(first, end):
-                        raw2[i] = piece[:, i - first, :]
+        for first, end in W2_LOADS:
+            raw2[first] = ring.tile([P, end - first, PACK * N], F32, name="raw2", tag="ring", align_bytes=64)
+            nc.sync.dma_start(
+                out=raw2[first][:], in_=w2[first:end].rearrange("e (p j) n -> p e (j n)", j=PACK)
+            )
         gates = {}
         for half in range(2):
             late = ring.tile([P, TOP - 1, HALF], F32, name="gate_late", tag="ring", align_bytes=64)
@@ -105,7 +103,7 @@ def tile_moe_ecr_glu_sigmoid_kernel(
             grouped = work.tile([P, PACK * H], BF16, name=name, align_bytes=64, bufs=3)
             copy(
                 grouped[:].rearrange("p (t a b j) -> p a j b t", t=PACK, b=2, j=PACK),
-                raw[:].rearrange("p j (a b t) -> p a j b t", b=2, t=PACK),
+                raw.rearrange("p (j a b t) -> p a j b t", j=PACK, b=2, t=PACK),
             )
             return grouped[:]
 
@@ -135,59 +133,57 @@ def tile_moe_ecr_glu_sigmoid_kernel(
 
         hidden = {}
 
-        banks = {}
-
         def first_layer(e):
-            grouped1 = round_first_layer(nc.scalar.copy, raw1[e], "grouped1")
-            grouped3 = round_first_layer(nc.vector.tensor_copy, raw3[e], "grouped3")
-            if e > 0:
-                gated_unit(e - 1, raw1[e][:, 0, :], raw3[e][:, 0, : C * PACK // 2].bitcast(BF16))
-            banks[e] = (
-                first_layer_product(e, quantize(work, grouped1, H, "w1", 2), "a_bank"),
-                first_layer_product(e, quantize(work, grouped3, H, "w3", 2), "b_bank"),
-            )
-
-        def gated_unit(e, sig, h):
-            a_bank, b_bank = banks[e]
-            sig_view = sig.rearrange("p (s t) -> p s t", t=PACK)
-            nc.scalar.activation(sig_view, a_bank[:].rearrange("p t s -> p s t"), SIGMOID)
+            grouped1 = round_first_layer(nc.vector.tensor_copy, raw1[e], "grouped1")
+            a_bank = first_layer_product(e, quantize(work, grouped1, H, "w1", 2), "a_bank")
+            grouped3 = round_first_layer(nc.scalar.copy, raw3[e], "grouped3")
+            sig = raw3[e][:, : C * PACK].rearrange("p (s t) -> p s t", t=PACK)
+            nc.scalar.activation(sig, a_bank[:].rearrange("p t s -> p s t"), SIGMOID)
+            b_bank = first_layer_product(e, quantize(work, grouped3, H, "w3", 2), "b_bank")
+            h = work.tile([P, C * PACK], BF16, name="h", align_bytes=64, bufs=2)
             nc.vector.tensor_tensor(
-                h.rearrange("p (s t) -> p s t", t=PACK), b_bank[:].rearrange("p t s -> p s t"), sig_view, MULT
+                h[:].rearrange("p (s t) -> p s t", t=PACK), b_bank[:].rearrange("p t s -> p s t"), sig, MULT
             )
-            hidden[e] = quantize(keep, h, C, "h%d" % e, 1)
-
-        def second_layer(first, end):
-            bank = psum.tile([P, end - first, C], F32, name="y_bank")
-            for e in range(first, end):
-                grouped = work.tile([P, PACK * N], BF16, name="grouped2", align_bytes=64)
-                copy = nc.vector.tensor_copy if e >= E // 2 and e % 2 == 1 else nc.scalar.copy
-                copy(
-                    grouped[:].rearrange("p (a i j) -> p a j i", i=4, j=PACK),
-                    raw2[e].rearrange("p (j a i) -> p a j i", j=PACK, i=4),
-                )
-                codes, scales = quantize(work, grouped[:], N, "w2", 4)
-                nc.tensor.matmul_mx(
-                    out=bank[:, e - first, :],
-                    lhsT=codes[:].bitcast(FP8X4),
-                    lhsT_scale=scales[:],
-                    rhs=hidden[e][0][:].bitcast(FP8X4),
-                    rhs_scale=hidden[e][1][:],
-                    start=True,
-                    stop=True,
-                )
-            nc.scalar.copy(y_slots[:, first * C : end * C], bank[:].rearrange("p e s -> p (e s)"))
+            hidden[e] = quantize(keep, h[:], C, "h%d" % e, 1)
 
         for e in range(E):
             if e % GATHER_EXPERTS == 0:
                 gather_tokens(e // GATHER_EXPERTS)
             first_layer(e)
-            if e == E - 1:
-                last_sig = keep.tile([P, C * PACK], F32, name="last_sig")
-                last_h = keep.tile([P, C * PACK], BF16, name="last_h", align_bytes=64)
-                gated_unit(e, last_sig[:], last_h[:])
-            for first, end, after in W2_PIECES:
-                if after == e:
-                    second_layer(first, end)
+
+        second_weights = {}
+
+        def quantize_second(first, end):
+            count = end - first
+            on_scalar = count == 2 and first % 4 == 0
+            copy = nc.scalar.copy if on_scalar else nc.vector.tensor_copy
+            grouped = work.tile([P, count * PACK * N], BF16, name="grouped2", align_bytes=64)
+            copy(
+                grouped[:].rearrange("p (e a i j) -> p e a j i", e=count, i=4, j=PACK),
+                raw2[first][:].rearrange("p e (j a i) -> p e a j i", j=PACK, i=4),
+            )
+            codes, scales = quantize(work, grouped[:], count * N, "w2", 4)
+            for e in range(first, end):
+                cols = slice((e - first) * N, (e - first + 1) * N)
+                second_weights[e] = (codes[:, cols], scales[:, cols])
+
+        for first, end in Y_BANKS:
+            bank = psum.tile([P, end - first, C], F32, name="y_bank", bufs=4)
+            for load in W2_LOADS:
+                if first <= load[0] < end:
+                    quantize_second(*load)
+                    for e in range(*load):
+                        nc.tensor.matmul_mx(
+                            out=bank[:, e - first, :],
+                            lhsT=second_weights[e][0].bitcast(FP8X4),
+                            lhsT_scale=second_weights[e][1],
+                            rhs=hidden[e][0][:].bitcast(FP8X4),
+                            rhs_scale=hidden[e][1][:],
+                            start=True,
+                            stop=True,
+                        )
+            copy = nc.vector.tensor_copy if end == E else nc.scalar.copy
+            copy(y_slots[:, first * C : end * C], bank[:].rearrange("p e s -> p (e s)"))
 
         def gated(r, half):
             product = keep.tile([P, HALF], F32, name="product%d_%d" % (r, half))

@@ -101,10 +101,10 @@ def tile_moe_ecr_glu_sigmoid_kernel(
 
         def round_first_layer(copy, raw, name):
             grouped = work.tile([P, PACK * H], BF16, name=name, align_bytes=64, bufs=3)
-            copy(
-                grouped[:].rearrange("p (t a b j) -> p a j b t", t=PACK, b=2, j=PACK),
-                raw.rearrange("p (j a b t) -> p a j b t", j=PACK, b=2, t=PACK),
-            )
+            target = grouped[:].rearrange("p (t a b j) -> p a j b t", t=PACK, b=2, j=PACK)
+            source = raw.rearrange("p (j a b t) -> p a j b t", j=PACK, b=2, t=PACK)
+            for t in range(0, PACK, 2):
+                copy(target[:, :, :, :, t : t + 2], source[:, :, :, :, t : t + 2])
             return grouped[:]
 
         def quantize(pool, grouped, width, name, bufs):

from contextlib import ExitStack

import concourse.mybir as mybir
from concourse.masks import make_identity

K, T, E, C, H, N = 512, 1024, 16, 128, 512, 128
TOP = 4
PAD = 64
SLOTS = E * C

FLOPS = 2 * SLOTS * (2 * K * H + H * N)

F32 = mybir.dt.float32
BF16 = mybir.dt.bfloat16
I32 = mybir.dt.int32
U32 = mybir.dt.uint32
U16 = mybir.dt.uint16
U8 = mybir.dt.uint8
FP8X4 = mybir.dt.float8_e4m3fn_x4
MULT = mybir.AluOpType.mult
ADD = mybir.AluOpType.add
SIGMOID = mybir.ActivationFunctionType.Sigmoid

P = 128
PACK = 4
STRIPE = 16
GATHER_EXPERTS = 4
RING = 12
HALF = T // 2
W2_LOADS = tuple((e, e + 2) for e in range(0, E - 2, 2)) + ((E - 2, E - 1), (E - 1, E))
Y_BANKS = ((0, 4), (4, 8), (8, 12), (12, 14), (14, 16))


def tile_moe_ecr_glu_sigmoid_kernel(
    tc, x_words, x_scales, w1, w3, w2, gate, offs, pos1, pos2, pos3, pos4, out
):
    nc = tc.nc
    with ExitStack() as ctx:
        keep = ctx.enter_context(tc.tile_pool(name="keep", bufs=1))
        ring = ctx.enter_context(tc.tile_pool(name="ring", bufs=RING))
        work = ctx.enter_context(tc.tile_pool(name="work", bufs=4))
        psum = ctx.enter_context(tc.psum_pool(name="psum", bufs=2))

        token_words = keep.tile([P, T], I32, name="token_words", align_bytes=64)
        token_scales = keep.tile([P, T], U8, name="token_scales", align_bytes=64)
        slot_list = keep.tile([P, SLOTS // STRIPE], U16, name="slot_list")
        scale_rows = keep.tile([P, T // 4], I32, name="scale_rows")
        nc.gpsimd.memset(token_scales[:].bitcast(I32), 0)
        nc.sync.dma_start(out=token_words[:], in_=x_words[0].rearrange("p t r -> p (t r)").bitcast(I32))
        nc.sync.dma_start(slot_list[:], offs)
        for r in range(4):
            nc.sync.dma_start(out=scale_rows[r:P:32, :], in_=x_scales[0, r:16:4, :].bitcast(I32))
        for q in range(4):
            live = slice(32 * q, 32 * q + 4)
            nc.vector.tensor_copy(token_scales[live, :].bitcast(I32), scale_rows[live, :])

        raw1, raw3, raw2 = {}, {}, {}
        pos_lists = []
        for e in range(E):
            for raw, w in ((raw1, w1), (raw3, w3)):
                piece = ring.tile([P, PACK * H], F32, name="raw", tag="ring", align_bytes=64)
                nc.sync.dma_start(out=piece[:], in_=w[e].rearrange("(p j) c -> p (j c)", j=PACK))
                raw[e] = piece[:]
            if e == 0:
                for r, pos in enumerate((pos1, pos2, pos3, pos4)):
                    pos_list = keep.tile([P, T // STRIPE], U16, name="pos_list%d" % r)
                    nc.sync.dma_start(pos_list[:], pos)
                    pos_lists.append(pos_list)
        for first, end in W2_LOADS:
            raw2[first] = ring.tile([P, end - first, PACK * N], F32, name="raw2", tag="ring", align_bytes=64)
            nc.sync.dma_start(
                out=raw2[first][:], in_=w2[first:end].rearrange("e (p j) n -> p e (j n)", j=PACK)
            )
        gates = {}
        for half in range(2):
            late = ring.tile([P, TOP - 1, HALF], F32, name="gate_late", tag="ring", align_bytes=64)
            nc.sync.dma_start(
                out=late[:], in_=gate[1:TOP, :, half * HALF : (half + 1) * HALF].rearrange("r p t -> p r t")
            )
            for r in range(1, TOP):
                gates[r, half] = late[:, r - 1, :]
        gate_first = ring.tile([P, T], F32, name="gate_first", tag="ring", align_bytes=64)
        nc.sync.dma_start(out=gate_first[:], in_=gate[0])
        for half in range(2):
            gates[0, half] = gate_first[:, half * HALF : (half + 1) * HALF]

        identity = keep.tile([P, P], F32, name="identity")
        make_identity(nc, identity[:])
        y_slots = keep.tile([P, SLOTS + PAD], F32, name="y_slots")
        nc.gpsimd.memset(y_slots[:, SLOTS:], 0.0)

        slot_words, slot_scales = {}, {}

        def gather_tokens(q):
            width = GATHER_EXPERTS * C
            entries = slot_list[:, q * width // STRIPE : (q + 1) * width // STRIPE]
            slot_words[q] = keep.tile([P, width], U32, name="slot_words%d" % q, align_bytes=64)
            slot_scales[q] = keep.tile([P, width], U8, name="slot_scales%d" % q, align_bytes=64)
            nc.vector.tensor_copy(slot_words[q][:], token_words[:].bitcast(U32).indirect(entries))
            nc.vector.tensor_copy(slot_scales[q][:], token_scales[:].indirect(entries))

        def round_first_layer(copy, raw, name):
            grouped = work.tile([P, PACK * H], BF16, name=name, align_bytes=64, bufs=3)
            target = grouped[:].rearrange("p (t a b j) -> p a j b t", t=PACK, b=2, j=PACK)
            source = raw.rearrange("p (j a b t) -> p a j b t", j=PACK, b=2, t=PACK)
            for t in range(0, PACK, 2):
                copy(target[:, :, :, :, t : t + 2], source[:, :, :, :, t : t + 2])
            return grouped[:]

        def quantize(pool, grouped, width, name, bufs):
            codes = pool.tile([P, width], U32, name=name + "_codes", align_bytes=64, bufs=bufs)
            scales = pool.tile([P, width], U8, name=name + "_scales", align_bytes=64, bufs=bufs)
            nc.vector.quantize_mx(out=codes[:].bitcast(FP8X4), scales=scales[:], in_=grouped)
            return codes, scales

        def first_layer_product(e, weights, name):
            codes, scales = weights
            q, place = divmod(e, GATHER_EXPERTS)
            slots = slice(place * C, (place + 1) * C)
            bank = psum.tile([P, PACK, C], F32, name=name)
            for t in range(PACK):
                cols = slice(t * P, (t + 1) * P)
                nc.tensor.matmul_mx(
                    out=bank[:, t, :],
                    lhsT=codes[:, cols].bitcast(FP8X4),
                    lhsT_scale=scales[:, cols],
                    rhs=slot_words[q][:, slots].bitcast(FP8X4),
                    rhs_scale=slot_scales[q][:, slots],
                    start=True,
                    stop=True,
                )
            return bank

        hidden = {}

        def first_layer(e):
            grouped1 = round_first_layer(nc.vector.tensor_copy, raw1[e], "grouped1")
            a_bank = first_layer_product(e, quantize(work, grouped1, H, "w1", 2), "a_bank")
            grouped3 = round_first_layer(nc.scalar.copy, raw3[e], "grouped3")
            sig = raw3[e][:, : C * PACK].rearrange("p (s t) -> p s t", t=PACK)
            nc.scalar.activation(sig, a_bank[:].rearrange("p t s -> p s t"), SIGMOID)
            b_bank = first_layer_product(e, quantize(work, grouped3, H, "w3", 2), "b_bank")
            h = work.tile([P, C * PACK], BF16, name="h", align_bytes=64, bufs=2)
            nc.vector.tensor_tensor(
                h[:].rearrange("p (s t) -> p s t", t=PACK), b_bank[:].rearrange("p t s -> p s t"), sig, MULT
            )
            hidden[e] = quantize(keep, h[:], C, "h%d" % e, 1)

        for e in range(E):
            if e % GATHER_EXPERTS == 0:
                gather_tokens(e // GATHER_EXPERTS)
            first_layer(e)

        second_weights = {}

        def quantize_second(first, end):
            count = end - first
            on_scalar = count == 2 and first % 4 == 0
            copy = nc.scalar.copy if on_scalar else nc.vector.tensor_copy
            grouped = work.tile([P, count * PACK * N], BF16, name="grouped2", align_bytes=64)
            copy(
                grouped[:].rearrange("p (e a i j) -> p e a j i", e=count, i=4, j=PACK),
                raw2[first][:].rearrange("p e (j a i) -> p e a j i", j=PACK, i=4),
            )
            codes, scales = quantize(work, grouped[:], count * N, "w2", 4)
            for e in range(first, end):
                cols = slice((e - first) * N, (e - first + 1) * N)
                second_weights[e] = (codes[:, cols], scales[:, cols])

        for first, end in Y_BANKS:
            bank = psum.tile([P, end - first, C], F32, name="y_bank", bufs=4)
            for load in W2_LOADS:
                if first <= load[0] < end:
                    quantize_second(*load)
                    for e in range(*load):
                        nc.tensor.matmul_mx(
                            out=bank[:, e - first, :],
                            lhsT=second_weights[e][0].bitcast(FP8X4),
                            lhsT_scale=second_weights[e][1],
                            rhs=hidden[e][0][:].bitcast(FP8X4),
                            rhs_scale=hidden[e][1][:],
                            start=True,
                            stop=True,
                        )
            copy = nc.vector.tensor_copy if end == E else nc.scalar.copy
            copy(y_slots[:, first * C : end * C], bank[:].rearrange("p e s -> p (e s)"))

        def gated(r, half):
            product = keep.tile([P, HALF], F32, name="product%d_%d" % (r, half))
            entries = pos_lists[r][:, half * HALF // STRIPE : (half + 1) * HALF // STRIPE]
            nc.vector.tensor_tensor(product[:], y_slots[:].indirect(entries), gates[r, half], MULT)
            return product

        blocks = HALF // P
        partial = {}
        for half in range(2):
            turned = psum.tile([P, blocks, P], F32, name="a_bank")
            order = list(range(TOP - 1, 0, -1))
            for r in order:
                product = gated(r, half)
                for b in range(blocks):
                    nc.tensor.matmul(
                        turned[:, b, :],
                        product[:, b * P : (b + 1) * P],
                        identity[:],
                        start=(r == order[0] and b == 0),
                        stop=(r == order[-1] and b == blocks - 1),
                        is_transpose=True,
                    )
            turned_sum = work.tile([P, blocks, P], F32, name="turned_sum", bufs=2)
            nc.scalar.copy(turned_sum[:], turned[:])
            partial[half] = psum.tile([P, blocks, P], F32, name="b_bank")
            for b in range(blocks):
                nc.tensor.transpose(partial[half][:, b, :], turned_sum[:, b, :], identity[:])
        for half in range(2):
            product = gated(0, half)
            result = work.tile([P, HALF], F32, name="result", bufs=2)
            nc.vector.tensor_tensor(result[:], partial[half][:].rearrange("p b t -> p (b t)"), product[:], ADD)
            nc.sync.dma_start(out=out[:, half * HALF : (half + 1) * HALF], in_=result[:])
